import numpy as np
CORES = [32,33,34,35,36,37,38,39,40,41,42,43,44,45,46,47,48,49,50,51,52,53,54,55,56,57,58,59,60,61,62,63]
N = 32
ROWS, COLS = 4, 8
def setup_inputs(rng):
    return {"x": rng.standard_normal((N, 128, 256), dtype=np.float32)}
def reference(x):
    g = x.astype(np.float64).reshape(ROWS, COLS, 128, 256)
    rs = g.sum(axis=1)
    cs = g.sum(axis=0)
    y1 = np.stack([rs[r // COLS] for r in range(N)]).astype(x.dtype)
    y2 = np.stack([cs[r % COLS] for r in range(N)]).astype(x.dtype)
    return {"y1": y1, "y2": y2}

@@ -1,0 +1,85 @@
+from concourse.bass import DstId, RemoteDMATransfer
+
+H = [128, 128]
+SCRATCH = {
+    "xs": ("dram", [2] + H, "float32"),
+    "l1": ("dram", [8] + H, "float32"),
+    "l2": ("dram", [4] + H, "float32"),
+    "p2": ("dram", [2] + H, "float32"),
+    "r1": ("dram", [2] + H, "float32"),
+    "r2": ("dram", [2] + H, "float32"),
+}
+SEMAPHORES = ["ld", "loc", "a1", "s1", "s2", "d1", "d2a", "d2b", "st1", "st2a", "st2b"]
+
+
+def rank_program(g, core, T, topo):
+    if T.rank_of(core) is None:
+        return
+    chip, k = core // 8, core % 8
+    mate, plane = chip ^ 1, chip ^ 2
+    gate = k in (2, 3, 6, 7)
+    S = T.sem
+
+    def did(ch, kk):
+        rid, pid = topo.addr(ch * 8 + kk)[:2]
+        return DstId(rid=rid, pnc=pid)
+
+    def xfer(srcs, dests, mask, sem):
+        return RemoteDMATransfer(dst_ids=[did(d[0], d[1]) for d in dests], dma_engine_mask=mask, remote_sem=sem,
+                                 srcs=srcs, dsts=[d[2] for d in dests], alu_op=1 if len(srcs) > 1 else 0)
+
+    sent = 0
+    g.sync.dma_start(T.xs[:], T.x[:]).then_inc(S.ld, 16)
+    g.wait_ge(S.ld, 16)
+
+    if gate:
+        w, own, far, slot = k ^ 1, chip & 1, mate, 2
+    else:
+        w, own, far, slot = k + 2, (chip >> 1) & 1, plane, 0
+    g.remote_dma_fused([
+        xfer([T.xs[1 - own]], [(far, w, T.l2[slot + 1])], 0x000F, S.s1),
+        xfer([T.xs[own]], [(chip, w, T.l2[slot])], 0x00F0, S.s1),
+        xfer([T.xs[0]], [(chip, j, T.l1[k]) for j in (0, 1) if j != k], 0x0F00, S.a1),
+        xfer([T.xs[1]], [(chip, j, T.l1[k]) for j in (4, 5) if j != k], 0xF000, S.a1),
+    ], local_sem=S.loc)
+    sent += 16
+
+    if not gate:
+        h = 0 if k < 2 else 1
+        rest = [j for j in range(8) if j not in (k, k ^ 1)]
+        dst = [k ^ 1] + rest[(k & 1)::2]
+        g.wait_ge(S.a1, 7 * 4)
+        g.remote_dma_fused([
+            xfer([T.xs[h]] + [T.l1[j] for j in range(8) if j != k], [(chip, j, T.r1[h]) for j in dst], 0xFFFF, S.d1),
+        ], local_sem=S.loc)
+        sent += 16
+    else:
+        h1, h2 = (chip >> 1) & 1, chip & 1
+        g.wait_ge(S.s1, 4 * 4)
+        g.remote_dma_fused([
+            xfer([T.l2[0], T.l2[1]], [(mate, k, T.p2[0])], 0x000F, S.s2),
+            xfer([T.l2[2], T.l2[3]], [(plane, k, T.p2[1])], 0x00F0, S.s2),
+        ], local_sem=S.loc)
+        sent += 8
+        g.wait_ge(S.s2, 2 * 4)
+        a = [T.l2[0], T.l2[1], T.p2[0]]
+        b = [T.l2[2], T.l2[3], T.p2[1]]
+        g.remote_dma_fused([
+            xfer(a, [(plane, k - 2, T.r2[h1])], 0x000F, S.d2b),
+            xfer(b, [(mate, k ^ 1, T.r2[h2])], 0x00F0, S.d2b),
+            xfer(a, [(chip, k - 2, T.r2[h1])], 0x0F00, S.d2a),
+            xfer(b, [(chip, k ^ 1, T.r2[h2])], 0xF000, S.d2a),
+        ], local_sem=S.loc)
+        sent += 16
+
+    g.sync.wait_ge(S.d1, 2 * 16)
+    g.sync.dma_start(T.y1[:], T.r1[:]).then_inc(S.st1, 16)
+    g.sync.wait_ge(S.d2a, 4)
+    g.sync.dma_start(T.y2[64 * own:64 * own + 64, :], T.r2[own]).then_inc(S.st2a, 16)
+    o = 1 - own
+    g.scalar.wait_ge(S.d2b, 4)
+    g.scalar.dma_start(T.y2[64 * o:64 * o + 64, :], T.r2[o]).then_inc(S.st2b, 16)
+    g.scalar.wait_ge(S.st2b, 16)
+    g.sync.wait_ge(S.st1, 16)
+    g.sync.wait_ge(S.st2a, 16)
+    g.wait_ge(S.loc, sent)

@@ -1,15 +1,15 @@
 from concourse.bass import DstId, RemoteDMATransfer
 
-H = [128, 128]
+Q = [128, 64]
 SCRATCH = {
-    "xs": ("dram", [2] + H, "float32"),
-    "l1": ("dram", [8] + H, "float32"),
-    "l2": ("dram", [4] + H, "float32"),
-    "p2": ("dram", [2] + H, "float32"),
-    "r1": ("dram", [2] + H, "float32"),
-    "r2": ("dram", [2] + H, "float32"),
+    "xs": ("dram", [4] + Q, "float32"),
+    "l1": ("dram", [16] + Q, "float32"),
+    "l2": ("dram", [8] + Q, "float32"),
+    "p2": ("dram", [4] + Q, "float32"),
+    "r1": ("dram", [4] + Q, "float32"),
+    "r2": ("dram", [4] + Q, "float32"),
 }
-SEMAPHORES = ["ld", "loc", "a1", "s1", "s2", "d1", "d2a", "d2b", "st1", "st2a", "st2b"]
+SEMAPHORES = ["ld", "loc", "a1", "s1a", "s1b", "s2a", "s2b", "d1", "da0", "da1", "db0", "db1", "sts", "stc"]
 
 
 def rank_program(g, core, T, topo):
@@ -36,13 +36,20 @@ def rank_program(g, core, T, topo):
         w, own, far, slot = k ^ 1, chip & 1, mate, 2
     else:
         w, own, far, slot = k + 2, (chip >> 1) & 1, plane, 0
+    o = 1 - own
     g.remote_dma_fused([
-        xfer([T.xs[1 - own]], [(far, w, T.l2[slot + 1])], 0x000F, S.s1),
-        xfer([T.xs[own]], [(chip, w, T.l2[slot])], 0x00F0, S.s1),
-        xfer([T.xs[0]], [(chip, j, T.l1[k]) for j in (0, 1) if j != k], 0x0F00, S.a1),
-        xfer([T.xs[1]], [(chip, j, T.l1[k]) for j in (4, 5) if j != k], 0xF000, S.a1),
+        xfer([T.xs[2 * o]], [(far, w, T.l2[2 * slot + 2])], 0x00FF, S.s1a),
+        xfer([T.xs[2 * own]], [(chip, w, T.l2[2 * slot])], 0xFF00, S.s1a),
     ], local_sem=S.loc)
-    sent += 16
+    g.remote_dma_fused([
+        xfer([T.xs[2 * o + 1]], [(far, w, T.l2[2 * slot + 3])], 0x000F, S.s1b),
+        xfer([T.xs[2 * own + 1]], [(chip, w, T.l2[2 * slot + 1])], 0x00F0, S.s1b),
+    ] + [
+        xfer([T.xs[q]], [(chip, j, T.l1[2 * k + q % 2]) for j in ((0, 1) if q < 2 else (4, 5)) if j != k],
+             0x0300 << (2 * q), S.a1)
+        for q in range(4)
+    ], local_sem=S.loc)
+    sent += 32
 
     if not gate:
         h = 0 if k < 2 else 1
@@ -50,36 +57,41 @@ def rank_program(g, core, T, topo):
         dst = [k ^ 1] + rest[(k & 1)::2]
         g.wait_ge(S.a1, 7 * 4)
         g.remote_dma_fused([
-            xfer([T.xs[h]] + [T.l1[j] for j in range(8) if j != k], [(chip, j, T.r1[h]) for j in dst], 0xFFFF, S.d1),
+            xfer([T.xs[2 * h + c]] + [T.l1[2 * j + c] for j in range(8) if j != k],
+                 [(chip, j, T.r1[2 * h + c]) for j in dst], 0x00FF << (8 * c), S.d1)
+            for c in range(2)
         ], local_sem=S.loc)
         sent += 16
     else:
         h1, h2 = (chip >> 1) & 1, chip & 1
-        g.wait_ge(S.s1, 4 * 4)
-        g.remote_dma_fused([
-            xfer([T.l2[0], T.l2[1]], [(mate, k, T.p2[0])], 0x000F, S.s2),
-            xfer([T.l2[2], T.l2[3]], [(plane, k, T.p2[1])], 0x00F0, S.s2),
-        ], local_sem=S.loc)
-        sent += 8
-        g.wait_ge(S.s2, 2 * 4)
-        a = [T.l2[0], T.l2[1], T.p2[0]]
-        b = [T.l2[2], T.l2[3], T.p2[1]]
-        g.remote_dma_fused([
-            xfer(a, [(plane, k - 2, T.r2[h1])], 0x000F, S.d2b),
-            xfer(b, [(mate, k ^ 1, T.r2[h2])], 0x00F0, S.d2b),
-            xfer(a, [(chip, k - 2, T.r2[h1])], 0x0F00, S.d2a),
-            xfer(b, [(chip, k ^ 1, T.r2[h2])], 0xF000, S.d2a),
-        ], local_sem=S.loc)
-        sent += 16
+        for c, sw, sn in ((0, S.s1a, S.s2a), (1, S.s1b, S.s2b)):
+            g.wait_ge(sw, 32 if c == 0 else 16)
+            g.remote_dma_fused([
+                xfer([T.l2[c], T.l2[2 + c]], [(mate, k, T.p2[c])], 0x000F, sn),
+                xfer([T.l2[4 + c], T.l2[6 + c]], [(plane, k, T.p2[2 + c])], 0x00F0, sn),
+            ], local_sem=S.loc)
+            sent += 8
+        for c, sw, near, away in ((0, S.s2a, S.da0, S.da1), (1, S.s2b, S.db0, S.db1)):
+            g.wait_ge(sw, 8)
+            a = [T.l2[c], T.l2[2 + c], T.p2[c]]
+            b = [T.l2[4 + c], T.l2[6 + c], T.p2[2 + c]]
+            g.remote_dma_fused([
+                xfer(a, [(plane, k - 2, T.r2[2 * h1 + c])], 0x000F, away),
+                xfer(b, [(mate, k ^ 1, T.r2[2 * h2 + c])], 0x00F0, away),
+                xfer(a, [(chip, k - 2, T.r2[2 * h1 + c])], 0x0F00, near),
+                xfer(b, [(chip, k ^ 1, T.r2[2 * h2 + c])], 0xF000, near),
+            ], local_sem=S.loc)
+            sent += 16
 
-    g.sync.wait_ge(S.d1, 2 * 16)
-    g.sync.dma_start(T.y1[:], T.r1[:]).then_inc(S.st1, 16)
-    g.sync.wait_ge(S.d2a, 4)
-    g.sync.dma_start(T.y2[64 * own:64 * own + 64, :], T.r2[own]).then_inc(S.st2a, 16)
-    o = 1 - own
-    g.scalar.wait_ge(S.d2b, 4)
-    g.scalar.dma_start(T.y2[64 * o:64 * o + 64, :], T.r2[o]).then_inc(S.st2b, 16)
-    g.scalar.wait_ge(S.st2b, 16)
-    g.sync.wait_ge(S.st1, 16)
-    g.sync.wait_ge(S.st2a, 16)
+    g.sync.wait_ge(S.d1, 4 * 8)
+    g.sync.dma_start(T.y1[:], T.r1[:]).then_inc(S.sts, 16)
+    for c, near, away in ((0, S.da0, S.da1), (1, S.db0, S.db1)):
+        q = 2 * own + c
+        g.sync.wait_ge(near, 4)
+        g.sync.dma_start(T.y2[32 * q:32 * q + 32, :], T.r2[q]).then_inc(S.sts, 16)
+        q = 2 * o + c
+        g.scalar.wait_ge(away, 4)
+        g.scalar.dma_start(T.y2[32 * q:32 * q + 32, :], T.r2[q]).then_inc(S.stc, 16)
+    g.sync.wait_ge(S.sts, 48)
+    g.scalar.wait_ge(S.stc, 32)
     g.wait_ge(S.loc, sent)

@@ -9,7 +9,8 @@ SCRATCH = {
     "r1": ("dram", [4] + Q, "float32"),
     "r2": ("dram", [4] + Q, "float32"),
 }
-SEMAPHORES = ["ld", "loc", "a1", "s1a", "s1b", "s2a", "s2b", "d1", "da0", "da1", "db0", "db1", "sts", "stc"]
+SEMAPHORES = ["lda", "ldb", "loc", "a1a", "a1b", "s1a", "s1b", "s2a", "s2b", "d1a", "d1b", "da", "db0", "db1",
+              "sts", "stc"]
 
 
 def rank_program(g, core, T, topo):
@@ -28,70 +29,78 @@ def rank_program(g, core, T, topo):
         return RemoteDMATransfer(dst_ids=[did(d[0], d[1]) for d in dests], dma_engine_mask=mask, remote_sem=sem,
                                  srcs=srcs, dsts=[d[2] for d in dests], alu_op=1 if len(srcs) > 1 else 0)
 
+    def qi(h, c):
+        return (1, 0)[c] if h == 0 else (2, 3)[c]
+
+    def rows(t, q, n=1):
+        return t[32 * q:32 * (q + n), :]
+
     sent = 0
-    g.sync.dma_start(T.xs[:], T.x[:]).then_inc(S.ld, 16)
-    g.wait_ge(S.ld, 16)
+    g.sync.dma_start(T.xs[1:3], rows(T.x, 1, 2)).then_inc(S.lda, 16)
+    g.scalar.dma_start(T.xs[0], rows(T.x, 0)).then_inc(S.ldb, 16)
+    g.sync.dma_start(T.xs[3], rows(T.x, 3)).then_inc(S.ldb, 16)
 
     if gate:
         w, own, far, slot = k ^ 1, chip & 1, mate, 2
     else:
         w, own, far, slot = k + 2, (chip >> 1) & 1, plane, 0
     o = 1 - own
-    g.remote_dma_fused([
-        xfer([T.xs[2 * o]], [(far, w, T.l2[2 * slot + 2])], 0x00FF, S.s1a),
-        xfer([T.xs[2 * own]], [(chip, w, T.l2[2 * slot])], 0xFF00, S.s1a),
-    ], local_sem=S.loc)
-    g.remote_dma_fused([
-        xfer([T.xs[2 * o + 1]], [(far, w, T.l2[2 * slot + 3])], 0x000F, S.s1b),
-        xfer([T.xs[2 * own + 1]], [(chip, w, T.l2[2 * slot + 1])], 0x00F0, S.s1b),
-    ] + [
-        xfer([T.xs[q]], [(chip, j, T.l1[2 * k + q % 2]) for j in ((0, 1) if q < 2 else (4, 5)) if j != k],
-             0x0300 << (2 * q), S.a1)
-        for q in range(4)
-    ], local_sem=S.loc)
-    sent += 32
+    for c, ld, n, s1, a1 in ((0, S.lda, 16, S.s1a, S.a1a), (1, S.ldb, 32, S.s1b, S.a1b)):
+        g.wait_ge(ld, n)
+        g.remote_dma_fused([
+            xfer([T.xs[qi(o, c)]], [(far, w, T.l2[2 * slot + 2 + c])], 0x000F, s1),
+            xfer([T.xs[qi(own, c)]], [(chip, w, T.l2[2 * slot + c])], 0x00F0, s1),
+            xfer([T.xs[qi(0, c)]], [(chip, j, T.l1[2 * k + c]) for j in (0, 1) if j != k], 0x0F00, a1),
+            xfer([T.xs[qi(1, c)]], [(chip, j, T.l1[2 * k + c]) for j in (4, 5) if j != k], 0xF000, a1),
+        ], local_sem=S.loc)
+        sent += 16
 
     if not gate:
         h = 0 if k < 2 else 1
         rest = [j for j in range(8) if j not in (k, k ^ 1)]
         dst = [k ^ 1] + rest[(k & 1)::2]
-        g.wait_ge(S.a1, 7 * 4)
-        g.remote_dma_fused([
-            xfer([T.xs[2 * h + c]] + [T.l1[2 * j + c] for j in range(8) if j != k],
-                 [(chip, j, T.r1[2 * h + c]) for j in dst], 0x00FF << (8 * c), S.d1)
-            for c in range(2)
-        ], local_sem=S.loc)
-        sent += 16
+        for c, a1, d1 in ((0, S.a1a, S.d1a), (1, S.a1b, S.d1b)):
+            g.wait_ge(a1, 7 * 4)
+            g.remote_dma_fused([
+                xfer([T.xs[qi(h, c)]] + [T.l1[2 * j + c] for j in range(8) if j != k],
+                     [(chip, j, T.r1[qi(h, c)]) for j in dst], 0xFFFF, d1),
+            ], local_sem=S.loc)
+            sent += 16
     else:
         h1, h2 = (chip >> 1) & 1, chip & 1
         for c, sw, sn in ((0, S.s1a, S.s2a), (1, S.s1b, S.s2b)):
-            g.wait_ge(sw, 32 if c == 0 else 16)
+            g.wait_ge(sw, 16)
             g.remote_dma_fused([
                 xfer([T.l2[c], T.l2[2 + c]], [(mate, k, T.p2[c])], 0x000F, sn),
                 xfer([T.l2[4 + c], T.l2[6 + c]], [(plane, k, T.p2[2 + c])], 0x00F0, sn),
             ], local_sem=S.loc)
             sent += 8
-        for c, sw, near, away in ((0, S.s2a, S.da0, S.da1), (1, S.s2b, S.db0, S.db1)):
+        for c, sw, near, away in ((0, S.s2a, S.da, S.da), (1, S.s2b, S.db0, S.db1)):
             g.wait_ge(sw, 8)
             a = [T.l2[c], T.l2[2 + c], T.p2[c]]
             b = [T.l2[4 + c], T.l2[6 + c], T.p2[2 + c]]
             g.remote_dma_fused([
-                xfer(a, [(plane, k - 2, T.r2[2 * h1 + c])], 0x000F, away),
-                xfer(b, [(mate, k ^ 1, T.r2[2 * h2 + c])], 0x00F0, away),
-                xfer(a, [(chip, k - 2, T.r2[2 * h1 + c])], 0x0F00, near),
-                xfer(b, [(chip, k ^ 1, T.r2[2 * h2 + c])], 0xF000, near),
+                xfer(a, [(plane, k - 2, T.r2[qi(h1, c)])], 0x000F, away),
+                xfer(b, [(mate, k ^ 1, T.r2[qi(h2, c)])], 0x00F0, away),
+                xfer(a, [(chip, k - 2, T.r2[qi(h1, c)])], 0x0F00, near),
+                xfer(b, [(chip, k ^ 1, T.r2[qi(h2, c)])], 0xF000, near),
             ], local_sem=S.loc)
             sent += 16
 
-    g.sync.wait_ge(S.d1, 4 * 8)
-    g.sync.dma_start(T.y1[:], T.r1[:]).then_inc(S.sts, 16)
-    for c, near, away in ((0, S.da0, S.da1), (1, S.db0, S.db1)):
-        q = 2 * own + c
-        g.sync.wait_ge(near, 4)
-        g.sync.dma_start(T.y2[32 * q:32 * q + 32, :], T.r2[q]).then_inc(S.sts, 16)
-        q = 2 * o + c
-        g.scalar.wait_ge(away, 4)
-        g.scalar.dma_start(T.y2[32 * q:32 * q + 32, :], T.r2[q]).then_inc(S.stc, 16)
-    g.sync.wait_ge(S.sts, 48)
+    g.sync.wait_ge(S.d1a, 32)
+    g.sync.dma_start(rows(T.y1, 1, 2), T.r1[1:3]).then_inc(S.sts, 16)
+    g.sync.wait_ge(S.d1b, 32)
+    g.sync.dma_start(rows(T.y1, 0), T.r1[0]).then_inc(S.sts, 16)
+    g.scalar.wait_ge(S.d1b, 32)
+    g.scalar.dma_start(rows(T.y1, 3), T.r1[3]).then_inc(S.stc, 16)
+    g.sync.wait_ge(S.da, 8)
+    g.sync.dma_start(rows(T.y2, 1, 2), T.r2[1:3]).then_inc(S.sts, 16)
+    q = qi(own, 1)
+    g.sync.wait_ge(S.db0, 4)
+    g.sync.dma_start(rows(T.y2, q), T.r2[q]).then_inc(S.sts, 16)
+    q = qi(o, 1)
+    g.scalar.wait_ge(S.db1, 4)
+    g.scalar.dma_start(rows(T.y2, q), T.r2[q]).then_inc(S.stc, 16)
+    g.sync.wait_ge(S.sts, 64)
     g.scalar.wait_ge(S.stc, 32)
     g.wait_ge(S.loc, sent)

from concourse.bass import DstId, RemoteDMATransfer

Q = [128, 64]
SCRATCH = {
    "xs": ("dram", [4] + Q, "float32"),
    "l1": ("dram", [16] + Q, "float32"),
    "l2": ("dram", [8] + Q, "float32"),
    "p2": ("dram", [4] + Q, "float32"),
    "r1": ("dram", [4] + Q, "float32"),
    "r2": ("dram", [4] + Q, "float32"),
}
SEMAPHORES = ["lda", "ldb", "loc", "a1a", "a1b", "s1a", "s1b", "s2a", "s2b", "d1a", "d1b", "da", "db0", "db1",
              "sts", "stc"]


def rank_program(g, core, T, topo):
    if T.rank_of(core) is None:
        return
    chip, k = core // 8, core % 8
    mate, plane = chip ^ 1, chip ^ 2
    gate = k in (2, 3, 6, 7)
    S = T.sem

    def did(ch, kk):
        rid, pid = topo.addr(ch * 8 + kk)[:2]
        return DstId(rid=rid, pnc=pid)

    def xfer(srcs, dests, mask, sem):
        return RemoteDMATransfer(dst_ids=[did(d[0], d[1]) for d in dests], dma_engine_mask=mask, remote_sem=sem,
                                 srcs=srcs, dsts=[d[2] for d in dests], alu_op=1 if len(srcs) > 1 else 0)

    def qi(h, c):
        return (1, 0)[c] if h == 0 else (2, 3)[c]

    def rows(t, q, n=1):
        return t[32 * q:32 * (q + n), :]

    sent = 0
    g.sync.dma_start(T.xs[1:3], rows(T.x, 1, 2)).then_inc(S.lda, 16)
    g.scalar.dma_start(T.xs[0], rows(T.x, 0)).then_inc(S.ldb, 16)
    g.sync.dma_start(T.xs[3], rows(T.x, 3)).then_inc(S.ldb, 16)

    if gate:
        w, own, far, slot = k ^ 1, chip & 1, mate, 2
    else:
        w, own, far, slot = k + 2, (chip >> 1) & 1, plane, 0
    o = 1 - own
    for c, ld, n, s1, a1 in ((0, S.lda, 16, S.s1a, S.a1a), (1, S.ldb, 32, S.s1b, S.a1b)):
        g.wait_ge(ld, n)
        g.remote_dma_fused([
            xfer([T.xs[qi(o, c)]], [(far, w, T.l2[2 * slot + 2 + c])], 0x000F, s1),
            xfer([T.xs[qi(own, c)]], [(chip, w, T.l2[2 * slot + c])], 0x00F0, s1),
            xfer([T.xs[qi(0, c)]], [(chip, j, T.l1[2 * k + c]) for j in (0, 1) if j != k], 0x0F00, a1),
            xfer([T.xs[qi(1, c)]], [(chip, j, T.l1[2 * k + c]) for j in (4, 5) if j != k], 0xF000, a1),
        ], local_sem=S.loc)
        sent += 16

    if not gate:
        h = 0 if k < 2 else 1
        rest = [j for j in range(8) if j not in (k, k ^ 1)]
        dst = [k ^ 1] + rest[(k & 1)::2]
        for c, a1, d1 in ((0, S.a1a, S.d1a), (1, S.a1b, S.d1b)):
            g.wait_ge(a1, 7 * 4)
            g.remote_dma_fused([
                xfer([T.xs[qi(h, c)]] + [T.l1[2 * j + c] for j in range(8) if j != k],
                     [(chip, j, T.r1[qi(h, c)]) for j in dst], 0xFFFF, d1),
            ], local_sem=S.loc)
            sent += 16
    else:
        h1, h2 = (chip >> 1) & 1, chip & 1
        for c, sw, sn in ((0, S.s1a, S.s2a), (1, S.s1b, S.s2b)):
            g.wait_ge(sw, 16)
            g.remote_dma_fused([
                xfer([T.l2[c], T.l2[2 + c]], [(mate, k, T.p2[c])], 0x000F, sn),
                xfer([T.l2[4 + c], T.l2[6 + c]], [(plane, k, T.p2[2 + c])], 0x00F0, sn),
            ], local_sem=S.loc)
            sent += 8
        for c, sw, near, away in ((0, S.s2a, S.da, S.da), (1, S.s2b, S.db0, S.db1)):
            g.wait_ge(sw, 8)
            a = [T.l2[c], T.l2[2 + c], T.p2[c]]
            b = [T.l2[4 + c], T.l2[6 + c], T.p2[2 + c]]
            g.remote_dma_fused([
                xfer(a, [(plane, k - 2, T.r2[qi(h1, c)])], 0x000F, away),
                xfer(b, [(mate, k ^ 1, T.r2[qi(h2, c)])], 0x00F0, away),
                xfer(a, [(chip, k - 2, T.r2[qi(h1, c)])], 0x0F00, near),
                xfer(b, [(chip, k ^ 1, T.r2[qi(h2, c)])], 0xF000, near),
            ], local_sem=S.loc)
            sent += 16

    g.sync.wait_ge(S.d1a, 32)
    g.sync.dma_start(rows(T.y1, 1, 2), T.r1[1:3]).then_inc(S.sts, 16)
    g.sync.wait_ge(S.d1b, 32)
    g.sync.dma_start(rows(T.y1, 0), T.r1[0]).then_inc(S.sts, 16)
    g.scalar.wait_ge(S.d1b, 32)
    g.scalar.dma_start(rows(T.y1, 3), T.r1[3]).then_inc(S.stc, 16)
    g.sync.wait_ge(S.da, 8)
    g.sync.dma_start(rows(T.y2, 1, 2), T.r2[1:3]).then_inc(S.sts, 16)
    q = qi(own, 1)
    g.sync.wait_ge(S.db0, 4)
    g.sync.dma_start(rows(T.y2, q), T.r2[q]).then_inc(S.sts, 16)
    q = qi(o, 1)
    g.scalar.wait_ge(S.db1, 4)
    g.scalar.dma_start(rows(T.y2, q), T.r2[q]).then_inc(S.stc, 16)
    g.sync.wait_ge(S.sts, 64)
    g.scalar.wait_ge(S.stc, 32)
    g.wait_ge(S.loc, sent)
